import numpy as np
import ml_dtypes


def mxq(x, axis, fmt="e4m3"):
    dtype, down = {"e4m3": (ml_dtypes.float8_e4m3fn, 7), "e5m2": (ml_dtypes.float8_e5m2, 14)}[fmt]
    v = np.moveaxis(np.asarray(x, np.float32).astype(ml_dtypes.bfloat16).astype(np.float64), axis, -1)
    blocks = v.reshape(v.shape[:-1] + (-1, 32))
    amax = np.abs(blocks).max(-1, keepdims=True)
    byte = np.maximum(np.where(amax > 0, np.frexp(amax)[1] - 1 + 127, 0) - down, 1)
    scale = np.exp2(byte - 127.0)
    codes = (blocks / scale).astype(np.float32).astype(dtype).astype(np.float64)
    return np.moveaxis((codes * scale).reshape(v.shape), -1, axis)


WIDE = False


def mx_kscale(k):
    if not WIDE:
        return np.ones(k)
    levels = np.array([10, -10, 5, -5, 0])
    if k % 512:
        return np.exp2(np.random.permutation(np.resize(levels, k // 32))).repeat(32)
    a = np.empty((k // 512, 16))
    for p in range(k // 512):
        a[p, :8] = np.random.permutation(np.resize(levels, 8))
        for g in range(8):
            far = levels[np.abs(levels - a[p, g]) >= 10]
            a[p, g + 8] = far[np.random.randint(len(far))]
    return np.exp2(a.ravel()).repeat(32)


def f64(x):
    return np.asarray(x).astype(np.float64)


def striped(idx):
    return np.tile(np.asarray(idx).reshape(-1, 16).T, (8, 1)).astype(np.uint16)


def unstriped(offs):
    return offs[:16].T.reshape(-1).astype(np.int64)


E2M1 = np.array([0.0, 0.5, 1.0, 1.5, 2.0, 3.0, 4.0, 6.0, -0.0, -0.5, -1.0, -1.5, -2.0, -3.0, -4.0, -6.0])


def pack_weight(w, fmt):
    k, n = w.shape
    w = f64(np.asarray(w, np.float32).astype(ml_dtypes.bfloat16)).reshape(k // 32, 32, n)
    amax = np.abs(w).max(1)
    if fmt == "e4m3":
        byte = np.frexp(amax)[1] - 1 + 127 - 7
    else:
        mant, ex = np.frexp(amax / 6.0)
        byte = np.where(mant > 0.5, ex, ex - 1) + 127
    byte = np.clip(np.where(amax > 0, byte, 1), 1, 254)
    scaled = (w * np.exp2(127.0 - byte)[:, None, :]).reshape(k, n).astype(np.float32)
    by_word = np.ascontiguousarray(scaled.reshape(k // 512, 128, 4, n).transpose(0, 1, 3, 2))
    if fmt == "e4m3":
        words = by_word.astype(ml_dtypes.float8_e4m3fn).view(np.uint8)
    else:
        c = by_word.astype(ml_dtypes.float4_e2m1fn).view(np.uint8) & 0xF
        words = (c[..., 0::2] | (c[..., 1::2] << 4)).reshape(k // 512, 128, 2 * n)
    return np.ascontiguousarray(words), np.ascontiguousarray(byte.astype(np.uint8).reshape(k // 512, 16, n))


def unpack_weight(words, scales, fmt):
    g, _, n = scales.shape
    words = np.ascontiguousarray(words).reshape(g, 128, n, -1)
    if fmt == "e4m3":
        vals = words.view(ml_dtypes.float8_e4m3fn).astype(np.float64)
    else:
        nib = np.empty((g, 128, n, 4), np.uint8)
        nib[..., 0::2] = words & 0xF
        nib[..., 1::2] = words >> 4
        vals = E2M1[nib]
    vals = vals * np.repeat(np.exp2(scales.astype(np.float64) - 127.0), 8, axis=1)[..., None]
    return vals.transpose(0, 1, 3, 2).reshape(g * 512, n)


D, T, I, Q, E, V = 512, 2048, 512, 256, 512, 32


def setup_inputs():
    n = np.random.standard_normal
    idx = np.random.permutation(T)[:I]
    idx2 = np.random.permutation(T)[:I]
    idx3 = np.random.permutation(Q)[:Q]
    idx4 = np.random.permutation(I)[:I]
    fd = mx_kscale(D)
    fi = mx_kscale(I)
    ti = np.ones(T)
    ti[idx] = fi
    keysp = pack_weight(n((D, T)) / fd[:, None], "e4m3")
    return {
        "query": (n((D, Q)) * 0.9 / np.sqrt(D) * fd[:, None]).astype(np.float32),
        "keys_words": keysp[0],
        "keys_scales": keysp[1],
        "lam": (np.random.uniform(0.5, 1.5, (1, Q))).astype(np.float32),
        "pull": (np.random.uniform(0.3, 0.8, (Q, 1))).astype(np.float32),
        "os": (np.random.uniform(4.0, 16.0, (1, I)) * fi).astype(np.float32),
        "vals": (n((E, T)) / ti).astype(np.float32),
        "hold": (np.random.uniform(0.3, 1.0, (1, Q))).astype(np.float32),
        "offs": striped(idx),
        "offs2": striped(idx2),
        "offs3": striped(idx3),
        "offs4": striped(idx4),
    }


def reference(query, keys_words, keys_scales, lam, pull, os, vals, hold, offs, offs2, offs3, offs4):
    idx = unstriped(offs)
    idx2 = unstriped(offs2)
    idx3 = unstriped(offs3)
    idx4 = unstriped(offs4)
    keysu = unpack_weight(keys_words, keys_scales, "e4m3")
    keysidxg = keysu[:, idx]
    queryq = mxq(f64(query), 0, "e4m3")
    a0 = keysidxg.T @ queryq
    keysidx2g = keysu[:, idx2]
    b0 = keysidx2g.T @ queryq
    vo = np.tanh(a0 - b0)
    vg = vo.reshape(I, V, Q // V).mean(axis=2)
    vr = np.repeat(vg, Q // V, axis=1)
    s0 = a0 + vr * f64(lam)
    s = s0.T
    p = np.exp(s - np.max(s, axis=1, keepdims=True))
    r = p / np.sum(p, axis=1, keepdims=True)
    dr0 = r - r[:, idx4]
    w = r - np.tanh(dr0 * 256.0) * f64(pull) / 256.0
    wo1 = w * f64(os)
    wt1 = wo1.T
    vt1 = f64(vals)[:, idx].T
    vt1q = mxq(vt1, 0, "e4m3")
    wt1q = mxq(wt1, 0, "e4m3")
    o = vt1q.T @ wt1q
    y = o - o[:, idx3] * f64(hold)
    return y

@@ -1,0 +1,266 @@
+from contextlib import ExitStack
+
+import concourse.mybir as mybir
+from concourse.masks import make_identity
+
+D, T, I, Q, E = 512, 2048, 512, 256, 512
+GROUP = 8
+FLOPS = 2 * (2 * D * I * Q + I * E * Q)
+
+F32 = mybir.dt.float32
+BF16 = mybir.dt.bfloat16
+I32 = mybir.dt.int32
+U32 = mybir.dt.uint32
+U16 = mybir.dt.uint16
+U8 = mybir.dt.uint8
+FP8X4 = mybir.dt.float8_e4m3fn_x4
+ALU = mybir.AluOpType
+ACT = mybir.ActivationFunctionType
+AXIS_X = mybir.AxisListType.X
+
+P = 128
+PACK = 4
+HALF = I // 2
+SPARE = 8
+
+
+def tile_attend_groupvotes_pulledback_comparedrows_kernel(
+    tc, query, keys_words, keys_scales, lam, pull, slot_factor, vals, hold, offs, offs2, offs3, offs4, out
+):
+    nc = tc.nc
+    q_tiles = Q // P
+    e_tiles = E // P
+
+    with ExitStack() as ctx:
+        lists = ctx.enter_context(tc.tile_pool(name="lists", bufs=1))
+        sb = ctx.enter_context(tc.tile_pool(name="sb", bufs=1))
+        ps = ctx.enter_context(tc.psum_pool(name="ps", bufs=1))
+
+        def sbuf(name, shape, dtype):
+            return sb.tile(shape, dtype, name=name, align_bytes=64)
+
+        def bank(name, tag, shape):
+            return ps.tile(shape, F32, name=name, tag=tag)
+
+        token_list = lists.tile([P, I // 16], U16, name="token_list")
+        rival_list = lists.tile([P, I // 16], U16, name="rival_list")
+        row_list = lists.tile([P, Q // 16], U16, name="row_list")
+        slot_list = lists.tile([P, I // 16], U16, name="slot_list")
+
+        pool_scales = sbuf("pool_scales", [P, T], U8)
+        nc.gpsimd.memset(pool_scales[:].bitcast(I32), 0)
+        nc.sync.dma_start(token_list[:], offs)
+        nc.sync.dma_start(rival_list[:], offs2)
+        q_raw = sbuf("q_raw", [P, PACK, Q], F32)
+        nc.sync.dma_start(out=q_raw[:], in_=query.rearrange("(p j) q -> p j q", j=PACK))
+        for quad in range(4):
+            nc.sync.dma_start(
+                out=pool_scales[32 * quad : 32 * quad + 4, :].bitcast(I32),
+                in_=keys_scales[0, 4 * quad : 4 * quad + 4, :].bitcast(I32),
+            )
+        pool_words = sbuf("pool_words", [P, T], I32)
+        nc.sync.dma_start(out=pool_words[:], in_=keys_words[0].rearrange("p n t -> p (n t)").bitcast(I32))
+
+        lam_pairs = sbuf("lam_pairs", [P, 2], F32)
+        nc.sync.dma_start(out=lam_pairs[:], in_=lam.rearrange("o (p h) -> p (o h)", h=2))
+        hold_pairs = sbuf("hold_pairs", [P, 2], F32)
+        nc.sync.dma_start(out=hold_pairs[:], in_=hold.rearrange("o (p h) -> p (o h)", h=2))
+        pool_vals = [sbuf(f"pool_vals{k}", [P, T], F32) for k in range(e_tiles)]
+        for k in range(2):
+            nc.sync.dma_start(out=pool_vals[k][:], in_=vals[k * P : (k + 1) * P, :])
+        nc.sync.dma_start(slot_list[:], offs4)
+        pull_cols = sbuf("pull_cols", [P, q_tiles], F32)
+        with nc.allow_non_contiguous_dma(reason="one pull value a partition and query tile"):
+            nc.sync.dma_start(out=pull_cols[:], in_=pull.rearrange("(h p) o -> p (h o)", p=P))
+        os_cols = sbuf("os_cols", [P, PACK], F32)
+        nc.sync.dma_start(out=os_cols[:], in_=slot_factor.rearrange("o (p t) -> p (o t)", t=PACK))
+        for k in range(2, e_tiles):
+            nc.sync.dma_start(out=pool_vals[k][:], in_=vals[k * P : (k + 1) * P, :])
+        nc.sync.dma_start(row_list[:], offs3)
+
+        ident = sbuf("ident", [P, P], F32)
+        make_identity(nc, ident[:])
+        o_sb = [sbuf(f"o_sb{k}", [P, Q + SPARE], F32) for k in range(e_tiles)]
+        for k in range(e_tiles):
+            nc.gpsimd.memset(o_sb[k][:, Q:], 0.0)
+
+        key_lists = (token_list, rival_list)
+        key_scales = [sbuf(f"key_scales{n}", [P, I], U8) for n in range(2)]
+        for n in range(2):
+            nc.vector.tensor_copy(key_scales[n][:], pool_scales[:].indirect(key_lists[n][:]))
+
+        q_bf = sbuf("q_bf", [P, Q, PACK], BF16)
+        nc.scalar.activation(
+            q_bf[:].rearrange("p (c i) t -> p c t i", i=4),
+            q_raw[:].rearrange("p t (c i) -> p c t i", i=4),
+            ACT.Copy,
+        )
+        q_codes = sbuf("q_codes", [P, Q], U32)
+        q_scales = sbuf("q_scales", [P, Q], U8)
+        nc.vector.quantize_mx(
+            out=q_codes[:].bitcast(FP8X4), scales=q_scales[:], in_=q_bf[:].rearrange("p q t -> p (q t)")
+        )
+
+        spread = bank("spread", "v0", [P, 4, P])
+        for h in range(2):
+            nc.tensor.transpose(spread[:, h, :], lam_pairs[:, h : h + 1].to_broadcast([P, P]), ident[:])
+        for h in range(2):
+            nc.tensor.transpose(spread[:, 2 + h, :], hold_pairs[:, h : h + 1].to_broadcast([P, P]), ident[:])
+        lam_row = sbuf("lam_row", [P, Q], F32)
+        nc.scalar.activation(
+            lam_row[:].rearrange("p (s h) -> p s h", h=2),
+            spread[:, 0:2, :].rearrange("p h s -> p s h"),
+            ACT.Copy,
+            scale=1.0 / GROUP,
+        )
+        hold_row = sbuf("hold_row", [P, Q], F32)
+        nc.scalar.copy(hold_row[:].rearrange("p (s h) -> p s h", h=2), spread[:, 2:4, :].rearrange("p h s -> p s h"))
+
+        products = [[bank(f"prod{n}{h}", f"{'ab'[n]}{h}", [P, 2, Q]) for h in range(2)] for n in range(2)]
+        a_sb = [sbuf(f"a_sb{h}", [P, 2, Q], F32) for h in range(2)]
+        for n in range(2):
+            for h in range(2):
+                words = sbuf(f"key_words{n}{h}", [P, HALF], U32)
+                nc.vector.tensor_copy(words[:], pool_words[:].bitcast(U32).indirect(key_lists[n][:, 16 * h : 16 * (h + 1)]))
+                for c in range(2):
+                    nc.tensor.matmul_mx(
+                        out=products[n][h][:, c, :],
+                        lhsT=words[:, c * P : (c + 1) * P].bitcast(FP8X4),
+                        lhsT_scale=key_scales[n][:, h * HALF + c * P : h * HALF + (c + 1) * P],
+                        rhs=q_codes[:].bitcast(FP8X4),
+                        rhs_scale=q_scales[:],
+                        start=True,
+                        stop=True,
+                    )
+                if n == 0:
+                    nc.scalar.copy(a_sb[h][:], products[0][h][:])
+
+        v_in = sbuf("v_in", [P, E, PACK], BF16)
+        v_codes = sbuf("v_codes", [P, E], U32)
+        v_scales = sbuf("v_scales", [P, E], U8)
+        w_codes = sbuf("w_codes", [P, Q], U32)
+        w_scales = sbuf("w_scales", [P, Q], U8)
+
+        def values(k):
+            cols = slice(k * P, (k + 1) * P)
+            picked = sbuf(f"v_picked{k}", [P, I], BF16)
+            nc.scalar.activation(picked[:], pool_vals[k][:].indirect(token_list[:]), ACT.Copy)
+            pairs = picked[:].bitcast(F32)
+            turned = bank(f"v_turned{k}", f"v{k % 2}", [P, 2, P])
+            for u in range(2):
+                nc.tensor.transpose(turned[:, u, :], pairs[:, u : I // 2 : 2], ident[:])
+            nc.vector.tensor_copy(v_in[:, cols, :].bitcast(F32), turned[:].rearrange("p u e -> p e u"))
+            nc.vector.quantize_mx(
+                out=v_codes[:, cols].bitcast(FP8X4),
+                scales=v_scales[:, cols],
+                in_=v_in[:, cols, :].rearrange("p e t -> p (e t)"),
+            )
+
+        def scores(g):
+            rows = slice(g * P, (g + 1) * P)
+            s_bank = bank(f"s_bank{g}", f"s{g}", [P, I])
+            for n in range(4):
+                nc.tensor.matmul(
+                    s_bank[:, n * P : (n + 1) * P], lhsT=a_sb[n // 2][:, n % 2, rows], rhs=ident[:],
+                    is_transpose=True, start=(n == 0), stop=False,
+                )
+            for h in range(2):
+                diff = sbuf(f"diff{g}{h}", [P, 2, P], F32)
+                nc.vector.tensor_tensor(diff[:], a_sb[h][:, :, rows], products[1][h][:, :, rows], ALU.subtract)
+                votes = sbuf(f"votes{g}{h}", [P, 2 * P], F32)
+                nc.scalar.activation(votes[:], diff[:].rearrange("p c q -> p (c q)"), ACT.Tanh)
+                sums = sbuf(f"vote_sums{g}{h}", [P, 2 * P // GROUP], F32)
+                nc.vector.tensor_reduce(sums[:], votes[:].rearrange("p (v j) -> p v j", j=GROUP), AXIS_X, ALU.add)
+                lift = sbuf(f"lift{g}{h}", [P, 2, P], F32)
+                shape = [P, 2, P // GROUP, GROUP]
+                nc.vector.tensor_tensor(
+                    lift[:].rearrange("p c (v j) -> p c v j", j=GROUP),
+                    sums[:].rearrange("p (c v) -> p c v", c=2).unsqueeze(3).broadcast_to(shape),
+                    lam_row[:, rows].rearrange("p (v j) -> p v j", j=GROUP).unsqueeze(1).broadcast_to(shape),
+                    ALU.mult,
+                )
+                for c in range(2):
+                    n = 2 * h + c
+                    nc.tensor.matmul(
+                        s_bank[:, n * P : (n + 1) * P], lhsT=lift[:, c, :], rhs=ident[:],
+                        is_transpose=True, start=False, stop=(n == 3),
+                    )
+            return s_bank
+
+        def weights(g, s_bank):
+            rows = slice(g * P, (g + 1) * P)
+            neg_max = sbuf(f"neg_max{g}", [P, 1], F32)
+            nc.vector.tensor_reduce(neg_max[:], s_bank[:], AXIS_X, ALU.max, negate=True)
+            p_tile = sbuf(f"p_tile{g}", [P, I], F32)
+            total = sbuf(f"total{g}", [P, 1], F32)
+            nc.scalar.activation(p_tile[:], s_bank[:], ACT.Exp, bias=neg_max[:], accum_out=total[:])
+            inv_total = sbuf(f"inv_total{g}", [P, 1], F32)
+            nc.vector.reciprocal(inv_total[:], total[:])
+            shares = sbuf(f"shares{g}", [P, I], F32)
+            nc.vector.tensor_scalar(shares[:], p_tile[:], inv_total[:], None, ALU.mult)
+
+            w_bank = bank(f"w_bank{g}", f"a{g}", [P, PACK, P])
+            for t in range(PACK):
+                nc.tensor.matmul(
+                    w_bank[:, t, :], lhsT=shares[:, t:I:PACK], rhs=ident[:],
+                    is_transpose=True, start=(t == 0), stop=False,
+                )
+            bent = sbuf(f"bent{g}", [P, PACK, P], F32)
+            pulled = sbuf(f"pulled{g}", [P, PACK, P], F32)
+            for h in range(2):
+                slots = slice(h * HALF, (h + 1) * HALF)
+                places = slice(h * P // 2, (h + 1) * P // 2)
+                named = sbuf(f"named{g}{h}", [P, HALF], F32)
+                nc.scalar.activation(named[:], shares[:].indirect(slot_list[:, 16 * h : 16 * (h + 1)]), ACT.Copy)
+                gap = sbuf(f"gap{g}{h}", [P, HALF], F32)
+                nc.vector.tensor_tensor(gap[:], shares[:, slots], named[:], ALU.subtract)
+                nc.scalar.activation(
+                    bent[:, :, places].rearrange("p t s -> p s t"),
+                    gap[:].rearrange("p (s t) -> p s t", t=PACK),
+                    ACT.Tanh,
+                    scale=256.0,
+                )
+                nc.vector.tensor_scalar(
+                    pulled[:, :, places], bent[:, :, places], pull_cols[:, g : g + 1], -1.0 / 256.0, ALU.mult, ALU.mult
+                )
+            for t in range(PACK):
+                nc.tensor.matmul(
+                    w_bank[:, t, :], lhsT=pulled[:, t, :], rhs=ident[:],
+                    is_transpose=True, start=False, stop=(t == PACK - 1),
+                )
+            w_in = sbuf(f"w_in{g}", [P, P, PACK], BF16)
+            nc.vector.tensor_tensor(
+                w_in[:],
+                w_bank[:].rearrange("p t q -> p q t"),
+                os_cols[:].unsqueeze(1).broadcast_to([P, P, PACK]),
+                ALU.mult,
+            )
+            nc.vector.quantize_mx(
+                out=w_codes[:, rows].bitcast(FP8X4), scales=w_scales[:, rows], in_=w_in[:].rearrange("p q t -> p (q t)")
+            )
+
+        s_banks = [scores(g) for g in range(q_tiles)]
+        for g in range(q_tiles):
+            weights(g, s_banks[g])
+        for k in range(e_tiles):
+            values(k)
+
+        o_tags = ("b0", "b1", "s0", "s1")
+        for k in range(e_tiles):
+            cols = slice(k * P, (k + 1) * P)
+            o_bank = bank(f"o_bank{k}", o_tags[k], [P, Q])
+            nc.tensor.matmul_mx(
+                out=o_bank[:],
+                lhsT=v_codes[:, cols].bitcast(FP8X4),
+                lhsT_scale=v_scales[:, cols],
+                rhs=w_codes[:].bitcast(FP8X4),
+                rhs_scale=w_scales[:],
+                start=True,
+                stop=True,
+            )
+            nc.scalar.copy(o_sb[k][:, :Q], o_bank[:])
+            taken = sbuf(f"taken{k}", [P, Q], F32)
+            nc.vector.tensor_tensor(taken[:], o_sb[k][:].indirect(row_list[:]), hold_row[:], ALU.mult)
+            result = sbuf(f"result{k}", [P, Q], F32)
+            nc.vector.tensor_tensor(result[:], o_sb[k][:, :Q], taken[:], ALU.subtract)
+            nc.sync.dma_start(out=out[cols, :], in_=result[:])

@@ -36,8 +36,8 @@ def tile_attend_groupvotes_pulledback_comparedrows_kernel(
         sb = ctx.enter_context(tc.tile_pool(name="sb", bufs=1))
         ps = ctx.enter_context(tc.psum_pool(name="ps", bufs=1))
 
-        def sbuf(name, shape, dtype):
-            return sb.tile(shape, dtype, name=name, align_bytes=64)
+        def sbuf(name, shape, dtype, tag=None):
+            return sb.tile(shape, dtype, name=name, tag=tag or name, align_bytes=64)
 
         def bank(name, tag, shape):
             return ps.tile(shape, F32, name=name, tag=tag)
@@ -51,20 +51,20 @@ def tile_attend_groupvotes_pulledback_comparedrows_kernel(
         nc.gpsimd.memset(pool_scales[:].bitcast(I32), 0)
         nc.sync.dma_start(token_list[:], offs)
         nc.sync.dma_start(rival_list[:], offs2)
-        q_raw = sbuf("q_raw", [P, PACK, Q], F32)
-        nc.sync.dma_start(out=q_raw[:], in_=query.rearrange("(p j) q -> p j q", j=PACK))
         for quad in range(4):
             nc.sync.dma_start(
                 out=pool_scales[32 * quad : 32 * quad + 4, :].bitcast(I32),
                 in_=keys_scales[0, 4 * quad : 4 * quad + 4, :].bitcast(I32),
             )
+        q_raw = sbuf("q_raw", [P, PACK, Q], F32)
+        nc.sync.dma_start(out=q_raw[:], in_=query.rearrange("(p j) q -> p j q", j=PACK))
         pool_words = sbuf("pool_words", [P, T], I32)
         nc.sync.dma_start(out=pool_words[:], in_=keys_words[0].rearrange("p n t -> p (n t)").bitcast(I32))
 
         lam_pairs = sbuf("lam_pairs", [P, 2], F32)
         nc.sync.dma_start(out=lam_pairs[:], in_=lam.rearrange("o (p h) -> p (o h)", h=2))
-        hold_pairs = sbuf("hold_pairs", [P, 2], F32)
-        nc.sync.dma_start(out=hold_pairs[:], in_=hold.rearrange("o (p h) -> p (o h)", h=2))
+        ident = sbuf("ident", [P, P], F32)
+        make_identity(nc, ident[:])
         pool_vals = [sbuf(f"pool_vals{k}", [P, T], F32) for k in range(e_tiles)]
         for k in range(2):
             nc.sync.dma_start(out=pool_vals[k][:], in_=vals[k * P : (k + 1) * P, :])
@@ -77,9 +77,9 @@ def tile_attend_groupvotes_pulledback_comparedrows_kernel(
         for k in range(2, e_tiles):
             nc.sync.dma_start(out=pool_vals[k][:], in_=vals[k * P : (k + 1) * P, :])
         nc.sync.dma_start(row_list[:], offs3)
+        hold_row = sbuf("hold_row", [P, Q], F32)
+        nc.sync.dma_start(out=hold_row[:], in_=hold.partition_broadcast(P))
 
-        ident = sbuf("ident", [P, P], F32)
-        make_identity(nc, ident[:])
         o_sb = [sbuf(f"o_sb{k}", [P, Q + SPARE], F32) for k in range(e_tiles)]
         for k in range(e_tiles):
             nc.gpsimd.memset(o_sb[k][:, Q:], 0.0)
@@ -101,27 +101,24 @@ def tile_attend_groupvotes_pulledback_comparedrows_kernel(
             out=q_codes[:].bitcast(FP8X4), scales=q_scales[:], in_=q_bf[:].rearrange("p q t -> p (q t)")
         )
 
-        spread = bank("spread", "v0", [P, 4, P])
+        spread = bank("spread", "v0", [P, 2, P])
         for h in range(2):
             nc.tensor.transpose(spread[:, h, :], lam_pairs[:, h : h + 1].to_broadcast([P, P]), ident[:])
-        for h in range(2):
-            nc.tensor.transpose(spread[:, 2 + h, :], hold_pairs[:, h : h + 1].to_broadcast([P, P]), ident[:])
         lam_row = sbuf("lam_row", [P, Q], F32)
         nc.scalar.activation(
             lam_row[:].rearrange("p (s h) -> p s h", h=2),
-            spread[:, 0:2, :].rearrange("p h s -> p s h"),
+            spread[:].rearrange("p h s -> p s h"),
             ACT.Copy,
             scale=1.0 / GROUP,
         )
-        hold_row = sbuf("hold_row", [P, Q], F32)
-        nc.scalar.copy(hold_row[:].rearrange("p (s h) -> p s h", h=2), spread[:, 2:4, :].rearrange("p h s -> p s h"))
 
         products = [[bank(f"prod{n}{h}", f"{'ab'[n]}{h}", [P, 2, Q]) for h in range(2)] for n in range(2)]
         a_sb = [sbuf(f"a_sb{h}", [P, 2, Q], F32) for h in range(2)]
+        key_words = sbuf("key_words", [P, 4, HALF], U32, tag="q_bf")
         for n in range(2):
             for h in range(2):
-                words = sbuf(f"key_words{n}{h}", [P, HALF], U32)
-                nc.vector.tensor_copy(words[:], pool_words[:].bitcast(U32).indirect(key_lists[n][:, 16 * h : 16 * (h + 1)]))
+                words = key_words[:, 2 * h + n, :]
+                nc.vector.tensor_copy(words, pool_words[:].bitcast(U32).indirect(key_lists[n][:, 16 * h : 16 * (h + 1)]))
                 for c in range(2):
                     nc.tensor.matmul_mx(
                         out=products[n][h][:, c, :],
@@ -141,12 +138,21 @@ def tile_attend_groupvotes_pulledback_comparedrows_kernel(
         w_codes = sbuf("w_codes", [P, Q], U32)
         w_scales = sbuf("w_scales", [P, Q], U8)
 
-        def values(k):
+        def pick(k):
+            picked = sbuf(f"v_picked{k}", [P, I], BF16, tag=("diff11","votes11","p_tile1","gap11")[k])
+            for h in range((1,1,1,1)[k]):
+                part = I // (1,1,1,1)[k]
+                listed = pool_vals[k][:].indirect(token_list[:, h * part // 16 : (h + 1) * part // 16])
+                if k in ():
+                    nc.vector.tensor_copy(picked[:, h * part : (h + 1) * part], listed)
+                else:
+                    nc.scalar.activation(picked[:, h * part : (h + 1) * part], listed, ACT.Copy)
+            return picked
+
+        def turn(k, picked):
             cols = slice(k * P, (k + 1) * P)
-            picked = sbuf(f"v_picked{k}", [P, I], BF16)
-            nc.scalar.activation(picked[:], pool_vals[k][:].indirect(token_list[:]), ACT.Copy)
             pairs = picked[:].bitcast(F32)
-            turned = bank(f"v_turned{k}", f"v{k % 2}", [P, 2, P])
+            turned = bank(f"v_turned{k}", ("s0","s1","v0","v1")[k], [P, 2, P])
             for u in range(2):
                 nc.tensor.transpose(turned[:, u, :], pairs[:, u : I // 2 : 2], ident[:])
             nc.vector.tensor_copy(v_in[:, cols, :].bitcast(F32), turned[:].rearrange("p u e -> p e u"))
@@ -187,8 +193,7 @@ def tile_attend_groupvotes_pulledback_comparedrows_kernel(
                     )
             return s_bank
 
-        def weights(g, s_bank):
-            rows = slice(g * P, (g + 1) * P)
+        def softmax(g, s_bank):
             neg_max = sbuf(f"neg_max{g}", [P, 1], F32)
             nc.vector.tensor_reduce(neg_max[:], s_bank[:], AXIS_X, ALU.max, negate=True)
             p_tile = sbuf(f"p_tile{g}", [P, I], F32)
@@ -198,7 +203,14 @@ def tile_attend_groupvotes_pulledback_comparedrows_kernel(
             nc.vector.reciprocal(inv_total[:], total[:])
             shares = sbuf(f"shares{g}", [P, I], F32)
             nc.vector.tensor_scalar(shares[:], p_tile[:], inv_total[:], None, ALU.mult)
+            own = None
+            if g in (0,1):
+                own = sbuf(f"own{g}", [P, I], F32)
+                nc.scalar.activation(own[:], p_tile[:], ACT.Copy, scale=inv_total[:])
+            return shares, own
 
+        def weights(g, shares, own):
+            rows = slice(g * P, (g + 1) * P)
             w_bank = bank(f"w_bank{g}", f"a{g}", [P, PACK, P])
             for t in range(PACK):
                 nc.tensor.matmul(
@@ -210,15 +222,18 @@ def tile_attend_groupvotes_pulledback_comparedrows_kernel(
             for h in range(2):
                 slots = slice(h * HALF, (h + 1) * HALF)
                 places = slice(h * P // 2, (h + 1) * P // 2)
-                named = sbuf(f"named{g}{h}", [P, HALF], F32)
-                nc.scalar.activation(named[:], shares[:].indirect(slot_list[:, 16 * h : 16 * (h + 1)]), ACT.Copy)
                 gap = sbuf(f"gap{g}{h}", [P, HALF], F32)
-                nc.vector.tensor_tensor(gap[:], shares[:, slots], named[:], ALU.subtract)
+                if g in (0,1):
+                    nc.vector.tensor_tensor(gap[:], shares[:].indirect(slot_list[:, 16 * h : 16 * (h + 1)]), own[:, slots], ALU.subtract)
+                else:
+                    named = sbuf(f"named{g}{h}", [P, HALF], F32)
+                    nc.scalar.activation(named[:], shares[:].indirect(slot_list[:, 16 * h : 16 * (h + 1)]), ACT.Copy)
+                    nc.vector.tensor_tensor(gap[:], named[:], shares[:, slots], ALU.subtract)
                 nc.scalar.activation(
                     bent[:, :, places].rearrange("p t s -> p s t"),
                     gap[:].rearrange("p (s t) -> p s t", t=PACK),
                     ACT.Tanh,
-                    scale=256.0,
+                    scale=-256.0,
                 )
                 nc.vector.tensor_scalar(
                     pulled[:, :, places], bent[:, :, places], pull_cols[:, g : g + 1], -1.0 / 256.0, ALU.mult, ALU.mult
@@ -240,12 +255,16 @@ def tile_attend_groupvotes_pulledback_comparedrows_kernel(
             )
 
         s_banks = [scores(g) for g in range(q_tiles)]
+        picked = [pick(0), pick(1)]
+        soft = [softmax(g, s_banks[g]) for g in range(q_tiles)]
+        picked.append(pick(2))
         for g in range(q_tiles):
-            weights(g, s_banks[g])
+            weights(g, *soft[g])
+        picked.append(pick(3))
         for k in range(e_tiles):
-            values(k)
+            turn(k, picked[k])
 
-        o_tags = ("b0", "b1", "s0", "s1")
+        o_tags = ("b0","b1","s0","s1")
         for k in range(e_tiles):
             cols = slice(k * P, (k + 1) * P)
             o_bank = bank(f"o_bank{k}", o_tags[k], [P, Q])
@@ -260,7 +279,12 @@ def tile_attend_groupvotes_pulledback_comparedrows_kernel(
             )
             nc.scalar.copy(o_sb[k][:, :Q], o_bank[:])
             taken = sbuf(f"taken{k}", [P, Q], F32)
-            nc.vector.tensor_tensor(taken[:], o_sb[k][:].indirect(row_list[:]), hold_row[:], ALU.mult)
+            if k in (2,3):
+                looked = sbuf(f"looked{k}", [P, Q], F32)
+                nc.scalar.activation(looked[:], o_sb[k][:].indirect(row_list[:]), ACT.Copy)
+                nc.vector.tensor_tensor(taken[:], looked[:], hold_row[:], ALU.mult)
+            else:
+                nc.vector.tensor_tensor(taken[:], o_sb[k][:].indirect(row_list[:]), hold_row[:], ALU.mult)
             result = sbuf(f"result{k}", [P, Q], F32)
             nc.vector.tensor_tensor(result[:], o_sb[k][:, :Q], taken[:], ALU.subtract)
             nc.sync.dma_start(out=out[cols, :], in_=result[:])

@@ -139,7 +139,7 @@ def tile_attend_groupvotes_pulledback_comparedrows_kernel(
         w_scales = sbuf("w_scales", [P, Q], U8)
 
         def pick(k):
-            picked = sbuf(f"v_picked{k}", [P, I], BF16, tag=("diff11","votes11","p_tile1","gap11")[k])
+            picked = sbuf(f"v_picked{k}", [P, I], BF16, tag=("diff11","votes01","p_tile1","gap11")[k])
             for h in range((1,1,1,1)[k]):
                 part = I // (1,1,1,1)[k]
                 listed = pool_vals[k][:].indirect(token_list[:, h * part // 16 : (h + 1) * part // 16])
@@ -155,7 +155,7 @@ def tile_attend_groupvotes_pulledback_comparedrows_kernel(
             turned = bank(f"v_turned{k}", ("s0","s1","v0","v1")[k], [P, 2, P])
             for u in range(2):
                 nc.tensor.transpose(turned[:, u, :], pairs[:, u : I // 2 : 2], ident[:])
-            nc.vector.tensor_copy(v_in[:, cols, :].bitcast(F32), turned[:].rearrange("p u e -> p e u"))
+            (nc.scalar.copy if k in (3,) else nc.vector.tensor_copy)(v_in[:, cols, :].bitcast(F32), turned[:].rearrange("p u e -> p e u"))
             nc.vector.quantize_mx(
                 out=v_codes[:, cols].bitcast(FP8X4),
                 scales=v_scales[:, cols],
@@ -175,7 +175,7 @@ def tile_attend_groupvotes_pulledback_comparedrows_kernel(
                 nc.vector.tensor_tensor(diff[:], a_sb[h][:, :, rows], products[1][h][:, :, rows], ALU.subtract)
                 votes = sbuf(f"votes{g}{h}", [P, 2 * P], F32)
                 nc.scalar.activation(votes[:], diff[:].rearrange("p c q -> p (c q)"), ACT.Tanh)
-                sums = sbuf(f"vote_sums{g}{h}", [P, 2 * P // GROUP], F32)
+                sums = sbuf(f"vote_sums{g}{h}", [P, 2 * P // GROUP], F32, tag="vote_sums01" if (g, h) == (1, 0) else None)
                 nc.vector.tensor_reduce(sums[:], votes[:].rearrange("p (v j) -> p v j", j=GROUP), AXIS_X, ALU.add)
                 lift = sbuf(f"lift{g}{h}", [P, 2, P], F32)
                 shape = [P, 2, P // GROUP, GROUP]

from contextlib import ExitStack

import concourse.mybir as mybir
from concourse.masks import make_identity

D, T, I, Q, E = 512, 2048, 512, 256, 512
GROUP = 8
FLOPS = 2 * (2 * D * I * Q + I * E * Q)

F32 = mybir.dt.float32
BF16 = mybir.dt.bfloat16
I32 = mybir.dt.int32
U32 = mybir.dt.uint32
U16 = mybir.dt.uint16
U8 = mybir.dt.uint8
FP8X4 = mybir.dt.float8_e4m3fn_x4
ALU = mybir.AluOpType
ACT = mybir.ActivationFunctionType
AXIS_X = mybir.AxisListType.X

P = 128
PACK = 4
HALF = I // 2
SPARE = 8


def tile_attend_groupvotes_pulledback_comparedrows_kernel(
    tc, query, keys_words, keys_scales, lam, pull, slot_factor, vals, hold, offs, offs2, offs3, offs4, out
):
    nc = tc.nc
    q_tiles = Q // P
    e_tiles = E // P

    with ExitStack() as ctx:
        lists = ctx.enter_context(tc.tile_pool(name="lists", bufs=1))
        sb = ctx.enter_context(tc.tile_pool(name="sb", bufs=1))
        ps = ctx.enter_context(tc.psum_pool(name="ps", bufs=1))

        def sbuf(name, shape, dtype, tag=None):
            return sb.tile(shape, dtype, name=name, tag=tag or name, align_bytes=64)

        def bank(name, tag, shape):
            return ps.tile(shape, F32, name=name, tag=tag)

        token_list = lists.tile([P, I // 16], U16, name="token_list")
        rival_list = lists.tile([P, I // 16], U16, name="rival_list")
        row_list = lists.tile([P, Q // 16], U16, name="row_list")
        slot_list = lists.tile([P, I // 16], U16, name="slot_list")

        pool_scales = sbuf("pool_scales", [P, T], U8)
        nc.gpsimd.memset(pool_scales[:].bitcast(I32), 0)
        nc.sync.dma_start(token_list[:], offs)
        nc.sync.dma_start(rival_list[:], offs2)
        for quad in range(4):
            nc.sync.dma_start(
                out=pool_scales[32 * quad : 32 * quad + 4, :].bitcast(I32),
                in_=keys_scales[0, 4 * quad : 4 * quad + 4, :].bitcast(I32),
            )
        q_raw = sbuf("q_raw", [P, PACK, Q], F32)
        nc.sync.dma_start(out=q_raw[:], in_=query.rearrange("(p j) q -> p j q", j=PACK))
        pool_words = sbuf("pool_words", [P, T], I32)
        nc.sync.dma_start(out=pool_words[:], in_=keys_words[0].rearrange("p n t -> p (n t)").bitcast(I32))

        lam_pairs = sbuf("lam_pairs", [P, 2], F32)
        nc.sync.dma_start(out=lam_pairs[:], in_=lam.rearrange("o (p h) -> p (o h)", h=2))
        ident = sbuf("ident", [P, P], F32)
        make_identity(nc, ident[:])
        pool_vals = [sbuf(f"pool_vals{k}", [P, T], F32) for k in range(e_tiles)]
        for k in range(2):
            nc.sync.dma_start(out=pool_vals[k][:], in_=vals[k * P : (k + 1) * P, :])
        nc.sync.dma_start(slot_list[:], offs4)
        pull_cols = sbuf("pull_cols", [P, q_tiles], F32)
        with nc.allow_non_contiguous_dma(reason="one pull value a partition and query tile"):
            nc.sync.dma_start(out=pull_cols[:], in_=pull.rearrange("(h p) o -> p (h o)", p=P))
        os_cols = sbuf("os_cols", [P, PACK], F32)
        nc.sync.dma_start(out=os_cols[:], in_=slot_factor.rearrange("o (p t) -> p (o t)", t=PACK))
        for k in range(2, e_tiles):
            nc.sync.dma_start(out=pool_vals[k][:], in_=vals[k * P : (k + 1) * P, :])
        nc.sync.dma_start(row_list[:], offs3)
        hold_row = sbuf("hold_row", [P, Q], F32)
        nc.sync.dma_start(out=hold_row[:], in_=hold.partition_broadcast(P))

        o_sb = [sbuf(f"o_sb{k}", [P, Q + SPARE], F32) for k in range(e_tiles)]
        for k in range(e_tiles):
            nc.gpsimd.memset(o_sb[k][:, Q:], 0.0)

        key_lists = (token_list, rival_list)
        key_scales = [sbuf(f"key_scales{n}", [P, I], U8) for n in range(2)]
        for n in range(2):
            nc.vector.tensor_copy(key_scales[n][:], pool_scales[:].indirect(key_lists[n][:]))

        q_bf = sbuf("q_bf", [P, Q, PACK], BF16)
        nc.scalar.activation(
            q_bf[:].rearrange("p (c i) t -> p c t i", i=4),
            q_raw[:].rearrange("p t (c i) -> p c t i", i=4),
            ACT.Copy,
        )
        q_codes = sbuf("q_codes", [P, Q], U32)
        q_scales = sbuf("q_scales", [P, Q], U8)
        nc.vector.quantize_mx(
            out=q_codes[:].bitcast(FP8X4), scales=q_scales[:], in_=q_bf[:].rearrange("p q t -> p (q t)")
        )

        spread = bank("spread", "v0", [P, 2, P])
        for h in range(2):
            nc.tensor.transpose(spread[:, h, :], lam_pairs[:, h : h + 1].to_broadcast([P, P]), ident[:])
        lam_row = sbuf("lam_row", [P, Q], F32)
        nc.scalar.activation(
            lam_row[:].rearrange("p (s h) -> p s h", h=2),
            spread[:].rearrange("p h s -> p s h"),
            ACT.Copy,
            scale=1.0 / GROUP,
        )

        products = [[bank(f"prod{n}{h}", f"{'ab'[n]}{h}", [P, 2, Q]) for h in range(2)] for n in range(2)]
        a_sb = [sbuf(f"a_sb{h}", [P, 2, Q], F32) for h in range(2)]
        key_words = sbuf("key_words", [P, 4, HALF], U32, tag="q_bf")
        for n in range(2):
            for h in range(2):
                words = key_words[:, 2 * h + n, :]
                nc.vector.tensor_copy(words, pool_words[:].bitcast(U32).indirect(key_lists[n][:, 16 * h : 16 * (h + 1)]))
                for c in range(2):
                    nc.tensor.matmul_mx(
                        out=products[n][h][:, c, :],
                        lhsT=words[:, c * P : (c + 1) * P].bitcast(FP8X4),
                        lhsT_scale=key_scales[n][:, h * HALF + c * P : h * HALF + (c + 1) * P],
                        rhs=q_codes[:].bitcast(FP8X4),
                        rhs_scale=q_scales[:],
                        start=True,
                        stop=True,
                    )
                if n == 0:
                    nc.scalar.copy(a_sb[h][:], products[0][h][:])

        v_in = sbuf("v_in", [P, E, PACK], BF16)
        v_codes = sbuf("v_codes", [P, E], U32)
        v_scales = sbuf("v_scales", [P, E], U8)
        w_codes = sbuf("w_codes", [P, Q], U32)
        w_scales = sbuf("w_scales", [P, Q], U8)

        def pick(k):
            picked = sbuf(f"v_picked{k}", [P, I], BF16, tag=("diff11","votes01","p_tile1","gap11")[k])
            for h in range((1,1,1,1)[k]):
                part = I // (1,1,1,1)[k]
                listed = pool_vals[k][:].indirect(token_list[:, h * part // 16 : (h + 1) * part // 16])
                if k in ():
                    nc.vector.tensor_copy(picked[:, h * part : (h + 1) * part], listed)
                else:
                    nc.scalar.activation(picked[:, h * part : (h + 1) * part], listed, ACT.Copy)
            return picked

        def turn(k, picked):
            cols = slice(k * P, (k + 1) * P)
            pairs = picked[:].bitcast(F32)
            turned = bank(f"v_turned{k}", ("s0","s1","v0","v1")[k], [P, 2, P])
            for u in range(2):
                nc.tensor.transpose(turned[:, u, :], pairs[:, u : I // 2 : 2], ident[:])
            (nc.scalar.copy if k in (3,) else nc.vector.tensor_copy)(v_in[:, cols, :].bitcast(F32), turned[:].rearrange("p u e -> p e u"))
            nc.vector.quantize_mx(
                out=v_codes[:, cols].bitcast(FP8X4),
                scales=v_scales[:, cols],
                in_=v_in[:, cols, :].rearrange("p e t -> p (e t)"),
            )

        def scores(g):
            rows = slice(g * P, (g + 1) * P)
            s_bank = bank(f"s_bank{g}", f"s{g}", [P, I])
            for n in range(4):
                nc.tensor.matmul(
                    s_bank[:, n * P : (n + 1) * P], lhsT=a_sb[n // 2][:, n % 2, rows], rhs=ident[:],
                    is_transpose=True, start=(n == 0), stop=False,
                )
            for h in range(2):
                diff = sbuf(f"diff{g}{h}", [P, 2, P], F32)
                nc.vector.tensor_tensor(diff[:], a_sb[h][:, :, rows], products[1][h][:, :, rows], ALU.subtract)
                votes = sbuf(f"votes{g}{h}", [P, 2 * P], F32)
                nc.scalar.activation(votes[:], diff[:].rearrange("p c q -> p (c q)"), ACT.Tanh)
                sums = sbuf(f"vote_sums{g}{h}", [P, 2 * P // GROUP], F32, tag="vote_sums01" if (g, h) == (1, 0) else None)
                nc.vector.tensor_reduce(sums[:], votes[:].rearrange("p (v j) -> p v j", j=GROUP), AXIS_X, ALU.add)
                lift = sbuf(f"lift{g}{h}", [P, 2, P], F32)
                shape = [P, 2, P // GROUP, GROUP]
                nc.vector.tensor_tensor(
                    lift[:].rearrange("p c (v j) -> p c v j", j=GROUP),
                    sums[:].rearrange("p (c v) -> p c v", c=2).unsqueeze(3).broadcast_to(shape),
                    lam_row[:, rows].rearrange("p (v j) -> p v j", j=GROUP).unsqueeze(1).broadcast_to(shape),
                    ALU.mult,
                )
                for c in range(2):
                    n = 2 * h + c
                    nc.tensor.matmul(
                        s_bank[:, n * P : (n + 1) * P], lhsT=lift[:, c, :], rhs=ident[:],
                        is_transpose=True, start=False, stop=(n == 3),
                    )
            return s_bank

        def softmax(g, s_bank):
            neg_max = sbuf(f"neg_max{g}", [P, 1], F32)
            nc.vector.tensor_reduce(neg_max[:], s_bank[:], AXIS_X, ALU.max, negate=True)
            p_tile = sbuf(f"p_tile{g}", [P, I], F32)
            total = sbuf(f"total{g}", [P, 1], F32)
            nc.scalar.activation(p_tile[:], s_bank[:], ACT.Exp, bias=neg_max[:], accum_out=total[:])
            inv_total = sbuf(f"inv_total{g}", [P, 1], F32)
            nc.vector.reciprocal(inv_total[:], total[:])
            shares = sbuf(f"shares{g}", [P, I], F32)
            nc.vector.tensor_scalar(shares[:], p_tile[:], inv_total[:], None, ALU.mult)
            own = None
            if g in (0,1):
                own = sbuf(f"own{g}", [P, I], F32)
                nc.scalar.activation(own[:], p_tile[:], ACT.Copy, scale=inv_total[:])
            return shares, own

        def weights(g, shares, own):
            rows = slice(g * P, (g + 1) * P)
            w_bank = bank(f"w_bank{g}", f"a{g}", [P, PACK, P])
            for t in range(PACK):
                nc.tensor.matmul(
                    w_bank[:, t, :], lhsT=shares[:, t:I:PACK], rhs=ident[:],
                    is_transpose=True, start=(t == 0), stop=False,
                )
            bent = sbuf(f"bent{g}", [P, PACK, P], F32)
            pulled = sbuf(f"pulled{g}", [P, PACK, P], F32)
            for h in range(2):
                slots = slice(h * HALF, (h + 1) * HALF)
                places = slice(h * P // 2, (h + 1) * P // 2)
                gap = sbuf(f"gap{g}{h}", [P, HALF], F32)
                if g in (0,1):
                    nc.vector.tensor_tensor(gap[:], shares[:].indirect(slot_list[:, 16 * h : 16 * (h + 1)]), own[:, slots], ALU.subtract)
                else:
                    named = sbuf(f"named{g}{h}", [P, HALF], F32)
                    nc.scalar.activation(named[:], shares[:].indirect(slot_list[:, 16 * h : 16 * (h + 1)]), ACT.Copy)
                    nc.vector.tensor_tensor(gap[:], named[:], shares[:, slots], ALU.subtract)
                nc.scalar.activation(
                    bent[:, :, places].rearrange("p t s -> p s t"),
                    gap[:].rearrange("p (s t) -> p s t", t=PACK),
                    ACT.Tanh,
                    scale=-256.0,
                )
                nc.vector.tensor_scalar(
                    pulled[:, :, places], bent[:, :, places], pull_cols[:, g : g + 1], -1.0 / 256.0, ALU.mult, ALU.mult
                )
            for t in range(PACK):
                nc.tensor.matmul(
                    w_bank[:, t, :], lhsT=pulled[:, t, :], rhs=ident[:],
                    is_transpose=True, start=False, stop=(t == PACK - 1),
                )
            w_in = sbuf(f"w_in{g}", [P, P, PACK], BF16)
            nc.vector.tensor_tensor(
                w_in[:],
                w_bank[:].rearrange("p t q -> p q t"),
                os_cols[:].unsqueeze(1).broadcast_to([P, P, PACK]),
                ALU.mult,
            )
            nc.vector.quantize_mx(
                out=w_codes[:, rows].bitcast(FP8X4), scales=w_scales[:, rows], in_=w_in[:].rearrange("p q t -> p (q t)")
            )

        s_banks = [scores(g) for g in range(q_tiles)]
        picked = [pick(0), pick(1)]
        soft = [softmax(g, s_banks[g]) for g in range(q_tiles)]
        picked.append(pick(2))
        for g in range(q_tiles):
            weights(g, *soft[g])
        picked.append(pick(3))
        for k in range(e_tiles):
            turn(k, picked[k])

        o_tags = ("b0","b1","s0","s1")
        for k in range(e_tiles):
            cols = slice(k * P, (k + 1) * P)
            o_bank = bank(f"o_bank{k}", o_tags[k], [P, Q])
            nc.tensor.matmul_mx(
                out=o_bank[:],
                lhsT=v_codes[:, cols].bitcast(FP8X4),
                lhsT_scale=v_scales[:, cols],
                rhs=w_codes[:].bitcast(FP8X4),
                rhs_scale=w_scales[:],
                start=True,
                stop=True,
            )
            nc.scalar.copy(o_sb[k][:, :Q], o_bank[:])
            taken = sbuf(f"taken{k}", [P, Q], F32)
            if k in (2,3):
                looked = sbuf(f"looked{k}", [P, Q], F32)
                nc.scalar.activation(looked[:], o_sb[k][:].indirect(row_list[:]), ACT.Copy)
                nc.vector.tensor_tensor(taken[:], looked[:], hold_row[:], ALU.mult)
            else:
                nc.vector.tensor_tensor(taken[:], o_sb[k][:].indirect(row_list[:]), hold_row[:], ALU.mult)
            result = sbuf(f"result{k}", [P, Q], F32)
            nc.vector.tensor_tensor(result[:], o_sb[k][:, :Q], taken[:], ALU.subtract)
            nc.sync.dma_start(out=out[cols, :], in_=result[:])
